import numpy as np
import ml_dtypes


def mxq(x, axis, fmt="e4m3"):
    dtype, down = {"e4m3": (ml_dtypes.float8_e4m3fn, 7), "e5m2": (ml_dtypes.float8_e5m2, 14)}[fmt]
    v = np.moveaxis(np.asarray(x, np.float32).astype(ml_dtypes.bfloat16).astype(np.float64), axis, -1)
    blocks = v.reshape(v.shape[:-1] + (-1, 32))
    amax = np.abs(blocks).max(-1, keepdims=True)
    byte = np.maximum(np.where(amax > 0, np.frexp(amax)[1] - 1 + 127, 0) - down, 1)
    scale = np.exp2(byte - 127.0)
    codes = (blocks / scale).astype(np.float32).astype(dtype).astype(np.float64)
    return np.moveaxis((codes * scale).reshape(v.shape), -1, axis)


WIDE = False


def mx_kscale(k):
    if not WIDE:
        return np.ones(k)
    levels = np.array([10, -10, 5, -5, 0])
    if k % 512:
        return np.exp2(np.random.permutation(np.resize(levels, k // 32))).repeat(32)
    a = np.empty((k // 512, 16))
    for p in range(k // 512):
        a[p, :8] = np.random.permutation(np.resize(levels, 8))
        for g in range(8):
            far = levels[np.abs(levels - a[p, g]) >= 10]
            a[p, g + 8] = far[np.random.randint(len(far))]
    return np.exp2(a.ravel()).repeat(32)


def f64(x):
    return np.asarray(x).astype(np.float64)


def striped8(idx):
    return np.asarray(idx).reshape(8, -1, 16).transpose(0, 2, 1).reshape(128, -1).astype(np.uint16)


def unstriped8(offs):
    return offs.reshape(8, 16, -1).transpose(0, 2, 1).reshape(8, -1).astype(np.int64)


def pick8(x, idx, run):
    r = np.arange(len(x))
    return x[r[:, None], idx[r % (8 * run) // run]]


E2M1 = np.array([0.0, 0.5, 1.0, 1.5, 2.0, 3.0, 4.0, 6.0, -0.0, -0.5, -1.0, -1.5, -2.0, -3.0, -4.0, -6.0])


def pack_weight(w, fmt):
    k, n = w.shape
    w = f64(np.asarray(w, np.float32).astype(ml_dtypes.bfloat16)).reshape(k // 32, 32, n)
    amax = np.abs(w).max(1)
    if fmt == "e4m3":
        byte = np.frexp(amax)[1] - 1 + 127 - 7
    else:
        mant, ex = np.frexp(amax / 6.0)
        byte = np.where(mant > 0.5, ex, ex - 1) + 127
    byte = np.clip(np.where(amax > 0, byte, 1), 1, 254)
    scaled = (w * np.exp2(127.0 - byte)[:, None, :]).reshape(k, n).astype(np.float32)
    by_word = np.ascontiguousarray(scaled.reshape(k // 512, 128, 4, n).transpose(0, 1, 3, 2))
    if fmt == "e4m3":
        words = by_word.astype(ml_dtypes.float8_e4m3fn).view(np.uint8)
    else:
        c = by_word.astype(ml_dtypes.float4_e2m1fn).view(np.uint8) & 0xF
        words = (c[..., 0::2] | (c[..., 1::2] << 4)).reshape(k // 512, 128, 2 * n)
    return np.ascontiguousarray(words), np.ascontiguousarray(byte.astype(np.uint8).reshape(k // 512, 16, n))


def unpack_weight(words, scales, fmt):
    g, _, n = scales.shape
    words = np.ascontiguousarray(words).reshape(g, 128, n, -1)
    if fmt == "e4m3":
        vals = words.view(ml_dtypes.float8_e4m3fn).astype(np.float64)
    else:
        nib = np.empty((g, 128, n, 4), np.uint8)
        nib[..., 0::2] = words & 0xF
        nib[..., 1::2] = words >> 4
        vals = E2M1[nib]
    vals = vals * np.repeat(np.exp2(scales.astype(np.float64) - 127.0), 8, axis=1)[..., None]
    return vals.transpose(0, 1, 3, 2).reshape(g * 512, n)


def sigmoid(v):
    return 1.0 / (1.0 + np.exp(-v))


D, T, U, X, I, Q, E = 512, 1024, 1024, 1024, 512, 512, 256


def setup_inputs():
    n = np.random.standard_normal
    idx = np.stack([np.random.permutation(T)[:I] for _ in range(8)])
    idx2 = np.stack([np.random.permutation(U)[:I] for _ in range(8)])
    idx3 = np.stack([np.random.permutation(X)[:I] for _ in range(8)])
    idx4 = np.stack([np.random.permutation(X)[:I] for _ in range(8)])
    fd = mx_kscale(D)
    fq = mx_kscale(Q)
    keysp = pack_weight(n((D, T)) / fd[:, None], "e2m1")
    notesp = pack_weight(n((D, U)) / fd[:, None], "e4m3")
    usersp = pack_weight(n((D, X)) / fd[:, None], "e4m3")
    mixp = pack_weight(n((Q, E)) * 1.0 / np.sqrt(Q) / fq[:, None], "e4m3")
    return {
        "query": (n((D, Q)) * 1.0 / np.sqrt(D) * fd[:, None]).astype(np.float32),
        "query2": (n((D, Q)) * 1.0 / np.sqrt(D) * fd[:, None]).astype(np.float32),
        "keys_words": keysp[0],
        "keys_scales": keysp[1],
        "notes_words": notesp[0],
        "notes_scales": notesp[1],
        "users_words": usersp[0],
        "users_scales": usersp[1],
        "thr": (np.random.uniform(-0.6, 0.6, (Q, 1))).astype(np.float32),
        "slope": (np.random.uniform(1.0, 3.0, (Q, 1))).astype(np.float32),
        "rowf": (np.random.uniform(0.5, 2.0, (Q, 1)) * fq[:, None]).astype(np.float32),
        "mix_words": mixp[0],
        "mix_scales": mixp[1],
        "offs": striped8(idx),
        "offs2": striped8(idx2),
        "offs3": striped8(idx3),
        "offs4": striped8(idx4),
    }


def reference(query, query2, keys_words, keys_scales, notes_words, notes_scales, users_words, users_scales, thr, slope, rowf, mix_words, mix_scales, offs, offs2, offs3, offs4):
    idx = unstriped8(offs)
    idx2 = unstriped8(offs2)
    idx3 = unstriped8(offs3)
    idx4 = unstriped8(offs4)
    keysu = unpack_weight(keys_words, keys_scales, "e2m1")
    notesu = unpack_weight(notes_words, notes_scales, "e4m3")
    usersu = unpack_weight(users_words, users_scales, "e4m3")
    mixu = unpack_weight(mix_words, mix_scales, "e4m3")
    queryq = mxq(f64(query), 0, "e4m3")
    a = queryq.T @ keysu
    b = queryq.T @ notesu
    query2q = mxq(f64(query2), 0, "e4m3")
    c0 = query2q.T @ usersu
    s1 = sigmoid(pick8(a, idx, 64) * f64(slope) + f64(thr))
    s2 = sigmoid(pick8(b, idx2, 64) * f64(slope) + f64(thr))
    r = s1 - s2
    f1 = np.zeros((Q, X))
    f1[np.arange(Q)[:, None], idx3[np.arange(Q) % 512 // 64]] = r
    cc = c0 + f1 * 3.0
    g = pick8(cc, idx4, 64)
    gw = g * f64(rowf)
    gwq = mxq(gw, 0, "e4m3")
    y = mixu.T @ gwq
    return y

@@ -1,0 +1,224 @@
+from contextlib import ExitStack
+
+import concourse.mybir as mybir
+
+D, T, I, Q, E = 512, 1024, 512, 512, 256
+FLOPS = 2 * (3 * D * Q * T + Q * E * I)
+
+F32 = mybir.dt.float32
+BF16 = mybir.dt.bfloat16
+I32 = mybir.dt.int32
+U32 = mybir.dt.uint32
+U16 = mybir.dt.uint16
+U8 = mybir.dt.uint8
+FP8X4 = mybir.dt.float8_e4m3fn_x4
+FP4X4 = mybir.dt.float4_e2m1fn_x4
+ALU = mybir.AluOpType
+ACT = mybir.ActivationFunctionType
+
+P = 128
+PACK = 4
+BANK = 512
+HALF = I // 2
+LIST_COLS = I // 16
+
+
+def tile_attend_gatedgap_threeq_mixed_kernel(
+    tc, query, query2, keys_words, keys_scales, notes_words, notes_scales, users_words, users_scales,
+    thr, slope, rowf, mix_words, mix_scales, offs, offs2, offs3, offs4, out,
+):
+    nc = tc.nc
+    with ExitStack() as ctx:
+        keep = ctx.enter_context(tc.tile_pool(name="keep", bufs=1))
+        psum = ctx.enter_context(tc.psum_pool(name="psum", bufs=1))
+
+        def scale_plane(name, width):
+            plane = keep.tile([P, width], U8, name=name, align_bytes=64)
+            return plane
+
+        def load_scales(plane, scales):
+            for quad in range(4):
+                nc.sync.dma_start(
+                    out=plane[32 * quad : 32 * quad + 4, :].bitcast(I32),
+                    in_=scales[0, 4 * quad : 4 * quad + 4, :].bitcast(I32),
+                )
+
+        def load_words(name, words, width):
+            held = keep.tile([P, width], U32, name=name, align_bytes=64)
+            nc.sync.dma_start(out=held[:].bitcast(I32), in_=words[0].rearrange("p n t -> p (n t)").bitcast(I32))
+            return held
+
+        def load_list(name, lists):
+            held = keep.tile([P, LIST_COLS], U16, name=name)
+            nc.sync.dma_start(held[:], lists)
+            return held
+
+        def load_rows(name, vec, queue):
+            held = keep.tile([P, PACK], F32, name=name)
+            queue.dma_start(out=held[:], in_=vec.rearrange("(p r) o -> p (r o)", r=PACK))
+            return held
+
+        def load_query(name, src, h):
+            raw = keep.tile([P, PACK, Q // 2], F32, name=f"{name}_raw{h}")
+            nc.sync.dma_start(out=raw[:], in_=src.rearrange("(p j) q -> p j q", j=PACK)[:, :, h * (Q // 2) : (h + 1) * (Q // 2)])
+            return raw
+
+        def dealt_views(grouped, raw, h):
+            dst = grouped[:].rearrange("p r m j -> p m j r")[:, h * (P // 2) : (h + 1) * (P // 2), :, :]
+            src = raw[:].rearrange("p j (m r) -> p m j r", r=PACK)
+            return dst, src
+
+        keys_plane = scale_plane("keys_plane", T)
+        notes_plane = scale_plane("notes_plane", T)
+        users_plane = scale_plane("users_plane", T)
+        mix_plane = scale_plane("mix_plane", E)
+        spread = keep.tile([P, T], F32, name="spread")
+        nc.vector.memset(spread[:], 0.0)
+
+        slope_sb = load_rows("slope_sb", slope, nc.gpsimd)
+        thr_sb = load_rows("thr_sb", thr, nc.gpsimd)
+
+        q_raw = [load_query("q", query, 0)]
+        load_scales(keys_plane, keys_scales)
+        q_raw.append(load_query("q", query, 1))
+        keys_sb = keep.tile([P, 2 * T], U8, name="keys_sb", align_bytes=64)
+        nc.sync.dma_start(out=keys_sb[:].bitcast(I32), in_=keys_words[0].bitcast(I32))
+        notes_sb = load_words("notes_sb", notes_words, T)
+        list1 = load_list("list1", offs)
+        load_scales(notes_plane, notes_scales)
+        list2 = load_list("list2", offs2)
+        q2_raw = [load_query("q2", query2, h) for h in range(2)]
+        list3 = load_list("list3", offs3)
+        users_sb = load_words("users_sb", users_words, T)
+        load_scales(users_plane, users_scales)
+        list4 = load_list("list4", offs4)
+        rowf_sb = load_rows("rowf_sb", rowf, nc.sync)
+        mix_sb = load_words("mix_sb", mix_words, E)
+        load_scales(mix_plane, mix_scales)
+
+        q_grouped = keep.tile([P, PACK, P, PACK], BF16, name="q_grouped", align_bytes=64)
+        q_codes = keep.tile([P, Q], U32, name="q_codes", align_bytes=64)
+        q_plane = keep.tile([P, Q], U8, name="q_plane", align_bytes=64)
+        for h in range(2):
+            dst, src = dealt_views(q_grouped, q_raw[h], h)
+            nc.vector.tensor_copy(out=dst, in_=src)
+        q_flat = q_grouped[:].rearrange("p r m j -> p (r m j)")
+        for c0, c1 in ((0, P), (P, Q)):
+            nc.vector.quantize_mx(out=q_codes[:, c0:c1].bitcast(FP8X4), scales=q_plane[:, c0:c1], in_=q_flat[:, PACK * c0 : PACK * c1])
+
+        q2_grouped = keep.tile([P, PACK, P, PACK], BF16, name="diff", align_bytes=64)
+        q2_codes = keep.tile([P, Q], U32, name="q2_codes", align_bytes=64)
+        q2_plane = keep.tile([P, Q], U8, name="q2_plane", align_bytes=64)
+
+        def scores(name, r, codes, plane, moving, moving_plane):
+            banks = psum.tile([P, 2, BANK], F32, name=f"{name}_banks")
+            rows = slice(r * P, (r + 1) * P)
+            for h in range(2):
+                nc.tensor.matmul_mx(
+                    out=banks[:, h, :], lhsT=codes[:, rows].bitcast(FP8X4), lhsT_scale=plane[:, rows],
+                    rhs=moving(h), rhs_scale=moving_plane[:, h * BANK : (h + 1) * BANK], start=True, stop=True,
+                )
+            return banks
+
+        def keys_half(h):
+            return keys_sb[:, 2 * h * BANK : 2 * (h + 1) * BANK].bitcast(FP4X4)
+
+        def notes_half(h):
+            return notes_sb[:, h * BANK : (h + 1) * BANK].bitcast(FP8X4)
+
+        def users_half(h):
+            return users_sb[:, h * BANK : (h + 1) * BANK].bitcast(FP8X4)
+
+        def copy_out(on_vector, dst, src):
+            if on_vector:
+                nc.vector.tensor_copy(out=dst, in_=src)
+            else:
+                nc.scalar.copy(out=dst, in_=src)
+
+        def fetch(name, r, moving, moving_plane):
+            banks = scores(name, r, q_codes, q_plane, moving, moving_plane)
+            whole = keep.tile([P, T], F32, name=f"window{(r + (name == 'b')) % 2}")
+            for h in range(2):
+                copy_out(r == 0, whole[:, h * BANK : (h + 1) * BANK], banks[:, h, :])
+            return whole
+
+        def windows(r):
+            return fetch("a", r, keys_half, keys_plane), fetch("b", r, notes_half, notes_plane)
+
+        def gates(r, pair):
+            made = []
+            for name, whole, lists in (("a", pair[0], list1), ("b", pair[1], list2)):
+                s = keep.tile([P, I], F32, name=f"{name}_gate{r}")
+                nc.scalar.activation(s[:], whole[:].indirect(lists[:]), ACT.Sigmoid, bias=thr_sb[:, r : r + 1], scale=slope_sb[:, r : r + 1])
+                made.append(s)
+            return made
+
+        def gap(r, made):
+            diff = keep.tile([P, I], F32, name="diff", align_bytes=64)
+            eng = nc.vector
+            eng.tensor_tensor(diff[:], made[0][:], made[1][:], ALU.subtract)
+            nc.vector.tensor_copy(spread[:].indirect(list3[:]), diff[:])
+
+        def add_users(r):
+            banks = scores("c", r, q2_codes, q2_plane, users_half, users_plane)
+            cc = keep.tile([P, T], F32, name=f"cc{r}")
+            for h in range(2):
+                cols = slice(h * BANK, (h + 1) * BANK)
+                nc.vector.scalar_tensor_tensor(cc[:, cols], spread[:, cols], 3.0, banks[:, h, :], ALU.mult, ALU.add)
+            return cc
+
+        gw_rows = keep.tile([P, 2, PACK, HALF], BF16, name="gw_rows")
+
+        def pick(r, cc, g):
+            nc.scalar.activation(g, cc[:].indirect(list4[:]), ACT.Copy)
+            nc.scalar.activation(gw_rows[:, :, r, :], g.rearrange("p (h i) -> p h i", h=2), ACT.Copy, scale=rowf_sb[:, r : r + 1])
+
+        made = gates(0, windows(0))
+        for h in range(2):
+            dst, src = dealt_views(q2_grouped, q2_raw[h], h)
+            nc.vector.tensor_copy(out=dst, in_=src)
+        nc.vector.quantize_mx(out=q2_codes[:].bitcast(FP8X4), scales=q2_plane[:], in_=q2_grouped[:].rearrange("p r m j -> p (r m j)"))
+        cc_all = []
+        for r in range(PACK):
+            gap(r, made)
+            cc_all.append(add_users(r))
+            if r + 1 < PACK:
+                made = gates(r + 1, windows(r + 1))
+        g_early = keep.tile([P, PACK - 1, I], F32, name="window0")
+        for r in range(PACK - 1):
+            pick(r, cc_all[r], g_early[:, r, :])
+
+        last = PACK - 1
+        cc = cc_all[last]
+        factor = rowf_sb[:, last : last + 1]
+        grouped = []
+        for h in range(2):
+            g = keep.tile([P, HALF], F32, name=f"g_last{h}")
+            picked = cc[:].indirect(list4[:, h * (LIST_COLS // 2) : (h + 1) * (LIST_COLS // 2)])
+            gw = keep.tile([P, HALF, PACK], BF16, name=f"gw{h}", align_bytes=64)
+            dst = gw[:].rearrange("p (c i) r -> p c r i", i=4)
+            src = gw_rows[:, h, :, :].rearrange("p r (c i) -> p c r i", i=4)
+            if h == 0:
+                nc.vector.tensor_copy(g[:], picked)
+                nc.vector.tensor_scalar(gw_rows[:, h, last, :], g[:], factor, None, ALU.mult)
+                nc.vector.tensor_copy(out=dst, in_=src)
+            else:
+                nc.scalar.activation(g[:], picked, ACT.Copy)
+                nc.scalar.activation(gw_rows[:, h, last, :], g[:], ACT.Copy, scale=factor)
+                nc.scalar.copy(out=dst, in_=src)
+            grouped.append(gw)
+
+        for h in range(2):
+            codes = keep.tile([P, HALF], U32, name=f"gw_codes{h}", align_bytes=64)
+            plane = keep.tile([P, HALF], U8, name=f"gw_plane{h}", align_bytes=64)
+            nc.vector.quantize_mx(out=codes[:].bitcast(FP8X4), scales=plane[:], in_=grouped[h][:].rearrange("p i r -> p (i r)"))
+            bank = psum.tile([P, 2, HALF], F32, name=f"out_bank{h}")
+            for t in range(E // P):
+                chans = slice(t * P, (t + 1) * P)
+                nc.tensor.matmul_mx(
+                    out=bank[:, t, :], lhsT=mix_sb[:, chans].bitcast(FP8X4), lhsT_scale=mix_plane[:, chans],
+                    rhs=codes[:].bitcast(FP8X4), rhs_scale=plane[:], start=True, stop=True,
+                )
+            result = keep.tile([P, 2, HALF], F32, name=f"result{h}")
+            copy_out(h == 1, result[:], bank[:])
+            nc.sync.dma_start(out=out.rearrange("(t p) i -> p t i", p=P)[:, :, h * HALF : (h + 1) * HALF], in_=result[:])

@@ -36,9 +36,9 @@ def tile_attend_gatedgap_threeq_mixed_kernel(
             plane = keep.tile([P, width], U8, name=name, align_bytes=64)
             return plane
 
-        def load_scales(plane, scales):
+        def load_scales(plane, scales, queue):
             for quad in range(4):
-                nc.sync.dma_start(
+                queue.dma_start(
                     out=plane[32 * quad : 32 * quad + 4, :].bitcast(I32),
                     in_=scales[0, 4 * quad : 4 * quad + 4, :].bitcast(I32),
                 )
@@ -72,53 +72,60 @@ def tile_attend_gatedgap_threeq_mixed_kernel(
         notes_plane = scale_plane("notes_plane", T)
         users_plane = scale_plane("users_plane", T)
         mix_plane = scale_plane("mix_plane", E)
-        spread = keep.tile([P, T], F32, name="spread")
-        nc.vector.memset(spread[:], 0.0)
+        spread = []
+        for n in range(2):
+            zeroed = keep.tile([P, T], F32, name=f"spread{n}")
+            nc.vector.memset(zeroed[:], 0.0)
+            spread.append(zeroed)
 
-        slope_sb = load_rows("slope_sb", slope, nc.gpsimd)
-        thr_sb = load_rows("thr_sb", thr, nc.gpsimd)
-
-        q_raw = [load_query("q", query, 0)]
-        load_scales(keys_plane, keys_scales)
-        q_raw.append(load_query("q", query, 1))
+        load_scales(keys_plane, keys_scales, nc.sync)
+        q_raw = [load_query("q", query, h) for h in range(2)]
         keys_sb = keep.tile([P, 2 * T], U8, name="keys_sb", align_bytes=64)
         nc.sync.dma_start(out=keys_sb[:].bitcast(I32), in_=keys_words[0].bitcast(I32))
         notes_sb = load_words("notes_sb", notes_words, T)
+        load_scales(notes_plane, notes_scales, nc.sync)
+        slope_sb = load_rows("slope_sb", slope, nc.sync)
+        thr_sb = load_rows("thr_sb", thr, nc.sync)
         list1 = load_list("list1", offs)
-        load_scales(notes_plane, notes_scales)
         list2 = load_list("list2", offs2)
         q2_raw = [load_query("q2", query2, h) for h in range(2)]
         list3 = load_list("list3", offs3)
         users_sb = load_words("users_sb", users_words, T)
-        load_scales(users_plane, users_scales)
+        load_scales(users_plane, users_scales, nc.sync)
         list4 = load_list("list4", offs4)
         rowf_sb = load_rows("rowf_sb", rowf, nc.sync)
         mix_sb = load_words("mix_sb", mix_words, E)
-        load_scales(mix_plane, mix_scales)
+        load_scales(mix_plane, mix_scales, nc.sync)
 
         q_grouped = keep.tile([P, PACK, P, PACK], BF16, name="q_grouped", align_bytes=64)
-        q_codes = keep.tile([P, Q], U32, name="q_codes", align_bytes=64)
+        q_first = keep.tile([P, P], U32, name="diff", align_bytes=64)
+        q_rest = keep.tile([P, Q - P], U32, name="q_rest", align_bytes=64)
         q_plane = keep.tile([P, Q], U8, name="q_plane", align_bytes=64)
         for h in range(2):
             dst, src = dealt_views(q_grouped, q_raw[h], h)
             nc.vector.tensor_copy(out=dst, in_=src)
         q_flat = q_grouped[:].rearrange("p r m j -> p (r m j)")
-        for c0, c1 in ((0, P), (P, Q)):
-            nc.vector.quantize_mx(out=q_codes[:, c0:c1].bitcast(FP8X4), scales=q_plane[:, c0:c1], in_=q_flat[:, PACK * c0 : PACK * c1])
+        nc.vector.quantize_mx(out=q_first[:].bitcast(FP8X4), scales=q_plane[:, :P], in_=q_flat[:, : PACK * P])
+        nc.vector.quantize_mx(out=q_rest[:].bitcast(FP8X4), scales=q_plane[:, P:], in_=q_flat[:, PACK * P :])
 
-        q2_grouped = keep.tile([P, PACK, P, PACK], BF16, name="diff", align_bytes=64)
-        q2_codes = keep.tile([P, Q], U32, name="q2_codes", align_bytes=64)
+        q2_first = keep.tile([P, P], U32, name="q2_first", align_bytes=64)
+        q2_rest = keep.tile([P, Q - P], U32, name="q2_rest", align_bytes=64)
         q2_plane = keep.tile([P, Q], U8, name="q2_plane", align_bytes=64)
 
-        def scores(name, r, codes, plane, moving, moving_plane):
-            banks = psum.tile([P, 2, BANK], F32, name=f"{name}_banks")
+        def bank_pair(name):
+            both = psum.tile([P, 2, BANK], F32, name=name)
+            return [both[:, h, :] for h in range(2)]
+
+        def single_banks(first):
+            return [psum.tile([P, BANK], F32, name=f"bank{first + h}")[:] for h in range(2)]
+
+        def scores(banks, r, codes, plane, moving, moving_plane):
             rows = slice(r * P, (r + 1) * P)
             for h in range(2):
                 nc.tensor.matmul_mx(
-                    out=banks[:, h, :], lhsT=codes[:, rows].bitcast(FP8X4), lhsT_scale=plane[:, rows],
+                    out=banks[h], lhsT=codes.bitcast(FP8X4), lhsT_scale=plane[:, rows],
                     rhs=moving(h), rhs_scale=moving_plane[:, h * BANK : (h + 1) * BANK], start=True, stop=True,
                 )
-            return banks
 
         def keys_half(h):
             return keys_sb[:, 2 * h * BANK : 2 * (h + 1) * BANK].bitcast(FP4X4)
@@ -136,10 +143,13 @@ def tile_attend_gatedgap_threeq_mixed_kernel(
                 nc.scalar.copy(out=dst, in_=src)
 
         def fetch(name, r, moving, moving_plane):
-            banks = scores(name, r, q_codes, q_plane, moving, moving_plane)
-            whole = keep.tile([P, T], F32, name=f"window{(r + (name == 'b')) % 2}")
+            slot = (r + (name == "b")) % 2
+            codes = q_first[:] if r == 0 else q_rest[:, (r - 1) * P : r * P]
+            banks = single_banks(2 * slot) if r == 0 else bank_pair(f"pair{slot}")
+            scores(banks, r, codes, q_plane, moving, moving_plane)
+            whole = keep.tile([P, T], F32, name="first_window" if (r, name) == (0, "a") else ("b_gate0", "window")[slot])
             for h in range(2):
-                copy_out(r == 0, whole[:, h * BANK : (h + 1) * BANK], banks[:, h, :])
+                copy_out(r == 0, whole[:, h * BANK : (h + 1) * BANK], banks[h])
             return whole
 
         def windows(r):
@@ -154,71 +164,76 @@ def tile_attend_gatedgap_threeq_mixed_kernel(
             return made
 
         def gap(r, made):
-            diff = keep.tile([P, I], F32, name="diff", align_bytes=64)
-            eng = nc.vector
-            eng.tensor_tensor(diff[:], made[0][:], made[1][:], ALU.subtract)
-            nc.vector.tensor_copy(spread[:].indirect(list3[:]), diff[:])
+            diff = keep.tile([P, I], F32, name=f"diff{r}")
+            engine = nc.vector if r == 0 else nc.gpsimd
+            engine.tensor_tensor(diff[:], made[0][:], made[1][:], ALU.subtract)
+            return diff
+
+        def scatter(r, diff):
+            nc.vector.tensor_copy(spread[r % 2][:].indirect(list3[:]), diff[:])
 
         def add_users(r):
-            banks = scores("c", r, q2_codes, q2_plane, users_half, users_plane)
+            codes = q2_first[:] if r == 0 else q2_rest[:, (r - 1) * P : r * P]
+            banks = single_banks(2 * r) if r < 2 else bank_pair(f"pair{(r + 1) % 2}")
+            scores(banks, r, codes, q2_plane, users_half, users_plane)
             cc = keep.tile([P, T], F32, name=f"cc{r}")
             for h in range(2):
                 cols = slice(h * BANK, (h + 1) * BANK)
-                nc.vector.scalar_tensor_tensor(cc[:, cols], spread[:, cols], 3.0, banks[:, h, :], ALU.mult, ALU.add)
+                nc.vector.scalar_tensor_tensor(cc[:, cols], spread[r % 2][:, cols], 3.0, banks[h], ALU.mult, ALU.add)
             return cc
 
-        gw_rows = keep.tile([P, 2, PACK, HALF], BF16, name="gw_rows")
+        gw = keep.tile([P, I, PACK], BF16, name="gw", align_bytes=64)
 
         def pick(r, cc, g):
+            factor = rowf_sb[:, r : r + 1]
             nc.scalar.activation(g, cc[:].indirect(list4[:]), ACT.Copy)
-            nc.scalar.activation(gw_rows[:, :, r, :], g.rearrange("p (h i) -> p h i", h=2), ACT.Copy, scale=rowf_sb[:, r : r + 1])
+            if r < 2:
+                nc.gpsimd.tensor_scalar(gw[:, :, r], g, factor, 0.0, ALU.mult, ALU.add)
+            else:
+                nc.scalar.activation(gw[:, :, r], g, ACT.Copy, scale=factor)
 
         made = gates(0, windows(0))
+        q2_grouped = keep.tile([P, PACK, P, PACK], BF16, name="diff", align_bytes=64)
         for h in range(2):
             dst, src = dealt_views(q2_grouped, q2_raw[h], h)
-            nc.vector.tensor_copy(out=dst, in_=src)
-        nc.vector.quantize_mx(out=q2_codes[:].bitcast(FP8X4), scales=q2_plane[:], in_=q2_grouped[:].rearrange("p r m j -> p (r m j)"))
+            if h == 0:
+                nc.vector.tensor_copy(out=dst, in_=src)
+            else:
+                nc.gpsimd.tensor_scalar(dst, src, 1.0, 0.0, ALU.mult, ALU.add)
+        q2_flat = q2_grouped[:].rearrange("p r m j -> p (r m j)")
+        nc.vector.quantize_mx(out=q2_first[:].bitcast(FP8X4), scales=q2_plane[:, :P], in_=q2_flat[:, : PACK * P])
+        nc.vector.quantize_mx(out=q2_rest[:].bitcast(FP8X4), scales=q2_plane[:, P:], in_=q2_flat[:, PACK * P :])
+        diff = gap(0, made)
         cc_all = []
         for r in range(PACK):
-            gap(r, made)
-            cc_all.append(add_users(r))
+            scatter(r, diff)
             if r + 1 < PACK:
-                made = gates(r + 1, windows(r + 1))
-        g_early = keep.tile([P, PACK - 1, I], F32, name="window0")
+                diff = gap(r + 1, gates(r + 1, windows(r + 1)))
+            cc_all.append(add_users(r))
+        g_early = keep.tile([P, PACK - 1, I], F32, name="b_gate0")
         for r in range(PACK - 1):
             pick(r, cc_all[r], g_early[:, r, :])
 
         last = PACK - 1
         cc = cc_all[last]
-        factor = rowf_sb[:, last : last + 1]
-        grouped = []
+        g_last = keep.tile([P, I], F32, name="b_gate0")
+        nc.vector.tensor_copy(g_last[:, :HALF], cc[:].indirect(list4[:, : LIST_COLS // 2]))
+        nc.scalar.activation(g_last[:, HALF:], cc[:].indirect(list4[:, LIST_COLS // 2 :]), ACT.Copy)
         for h in range(2):
-            g = keep.tile([P, HALF], F32, name=f"g_last{h}")
-            picked = cc[:].indirect(list4[:, h * (LIST_COLS // 2) : (h + 1) * (LIST_COLS // 2)])
-            gw = keep.tile([P, HALF, PACK], BF16, name=f"gw{h}", align_bytes=64)
-            dst = gw[:].rearrange("p (c i) r -> p c r i", i=4)
-            src = gw_rows[:, h, :, :].rearrange("p r (c i) -> p c r i", i=4)
-            if h == 0:
-                nc.vector.tensor_copy(g[:], picked)
-                nc.vector.tensor_scalar(gw_rows[:, h, last, :], g[:], factor, None, ALU.mult)
-                nc.vector.tensor_copy(out=dst, in_=src)
-            else:
-                nc.scalar.activation(g[:], picked, ACT.Copy)
-                nc.scalar.activation(gw_rows[:, h, last, :], g[:], ACT.Copy, scale=factor)
-                nc.scalar.copy(out=dst, in_=src)
-            grouped.append(gw)
+            slots = slice(h * HALF, (h + 1) * HALF)
+            nc.vector.tensor_scalar(gw[:, slots, last], g_last[:, slots], rowf_sb[:, last : last + 1], None, ALU.mult)
 
         for h in range(2):
             codes = keep.tile([P, HALF], U32, name=f"gw_codes{h}", align_bytes=64)
             plane = keep.tile([P, HALF], U8, name=f"gw_plane{h}", align_bytes=64)
-            nc.vector.quantize_mx(out=codes[:].bitcast(FP8X4), scales=plane[:], in_=grouped[h][:].rearrange("p i r -> p (i r)"))
-            bank = psum.tile([P, 2, HALF], F32, name=f"out_bank{h}")
+            nc.vector.quantize_mx(out=codes[:].bitcast(FP8X4), scales=plane[:], in_=gw[:, h * HALF : (h + 1) * HALF, :].rearrange("p i r -> p (i r)"))
+            banks = single_banks(2 * h)
             for t in range(E // P):
                 chans = slice(t * P, (t + 1) * P)
                 nc.tensor.matmul_mx(
-                    out=bank[:, t, :], lhsT=mix_sb[:, chans].bitcast(FP8X4), lhsT_scale=mix_plane[:, chans],
+                    out=banks[t][:, :HALF], lhsT=mix_sb[:, chans].bitcast(FP8X4), lhsT_scale=mix_plane[:, chans],
                     rhs=codes[:].bitcast(FP8X4), rhs_scale=plane[:], start=True, stop=True,
                 )
-            result = keep.tile([P, 2, HALF], F32, name=f"result{h}")
-            copy_out(h == 1, result[:], bank[:])
-            nc.sync.dma_start(out=out.rearrange("(t p) i -> p t i", p=P)[:, :, h * HALF : (h + 1) * HALF], in_=result[:])
+                result = keep.tile([P, HALF], F32, name=f"result{h}{t}")
+                copy_out(h == 1 and t == 1, result[:], banks[t][:, :HALF])
+                nc.sync.dma_start(out=out[chans, h * HALF : (h + 1) * HALF], in_=result[:])

@@ -21,6 +21,7 @@ PACK = 4
 BANK = 512
 HALF = I // 2
 LIST_COLS = I // 16
+GAP_WEIGHT = 3.0
 
 
 def tile_attend_gatedgap_threeq_mixed_kernel(
@@ -32,16 +33,14 @@ def tile_attend_gatedgap_threeq_mixed_kernel(
         keep = ctx.enter_context(tc.tile_pool(name="keep", bufs=1))
         psum = ctx.enter_context(tc.psum_pool(name="psum", bufs=1))
 
-        def scale_plane(name, width):
+        def load_scales(name, scales, width):
             plane = keep.tile([P, width], U8, name=name, align_bytes=64)
-            return plane
-
-        def load_scales(plane, scales, queue):
             for quad in range(4):
-                queue.dma_start(
+                nc.sync.dma_start(
                     out=plane[32 * quad : 32 * quad + 4, :].bitcast(I32),
                     in_=scales[0, 4 * quad : 4 * quad + 4, :].bitcast(I32),
                 )
+            return plane
 
         def load_words(name, words, width):
             held = keep.tile([P, width], U32, name=name, align_bytes=64)
@@ -53,77 +52,78 @@ def tile_attend_gatedgap_threeq_mixed_kernel(
             nc.sync.dma_start(held[:], lists)
             return held
 
-        def load_rows(name, vec, queue):
+        def load_rows(name, vec):
             held = keep.tile([P, PACK], F32, name=name)
-            queue.dma_start(out=held[:], in_=vec.rearrange("(p r) o -> p (r o)", r=PACK))
+            nc.sync.dma_start(out=held[:], in_=vec.rearrange("(p r) o -> p (r o)", r=PACK))
             return held
 
-        def load_query(name, src, h):
+        def load_query_half(name, src, h):
             raw = keep.tile([P, PACK, Q // 2], F32, name=f"{name}_raw{h}")
             nc.sync.dma_start(out=raw[:], in_=src.rearrange("(p j) q -> p j q", j=PACK)[:, :, h * (Q // 2) : (h + 1) * (Q // 2)])
             return raw
 
-        def dealt_views(grouped, raw, h):
-            dst = grouped[:].rearrange("p r m j -> p m j r")[:, h * (P // 2) : (h + 1) * (P // 2), :, :]
-            src = raw[:].rearrange("p j (m r) -> p m j r", r=PACK)
-            return dst, src
-
-        keys_plane = scale_plane("keys_plane", T)
-        notes_plane = scale_plane("notes_plane", T)
-        users_plane = scale_plane("users_plane", T)
-        mix_plane = scale_plane("mix_plane", E)
         spread = []
         for n in range(2):
             zeroed = keep.tile([P, T], F32, name=f"spread{n}")
             nc.vector.memset(zeroed[:], 0.0)
             spread.append(zeroed)
 
-        load_scales(keys_plane, keys_scales, nc.sync)
-        q_raw = [load_query("q", query, h) for h in range(2)]
+        keys_plane = load_scales("keys_plane", keys_scales, T)
+        q_raw = [load_query_half("q", query, h) for h in range(2)]
+        slope_sb = load_rows("slope_sb", slope)
+        thr_sb = load_rows("thr_sb", thr)
+        list1 = load_list("list1", offs)
         keys_sb = keep.tile([P, 2 * T], U8, name="keys_sb", align_bytes=64)
         nc.sync.dma_start(out=keys_sb[:].bitcast(I32), in_=keys_words[0].bitcast(I32))
         notes_sb = load_words("notes_sb", notes_words, T)
-        load_scales(notes_plane, notes_scales, nc.sync)
-        slope_sb = load_rows("slope_sb", slope, nc.sync)
-        thr_sb = load_rows("thr_sb", thr, nc.sync)
-        list1 = load_list("list1", offs)
+        notes_plane = load_scales("notes_plane", notes_scales, T)
         list2 = load_list("list2", offs2)
-        q2_raw = [load_query("q2", query2, h) for h in range(2)]
+        q2_raw = [load_query_half("q2", query2, h) for h in range(2)]
         list3 = load_list("list3", offs3)
         users_sb = load_words("users_sb", users_words, T)
-        load_scales(users_plane, users_scales, nc.sync)
+        users_plane = load_scales("users_plane", users_scales, T)
         list4 = load_list("list4", offs4)
-        rowf_sb = load_rows("rowf_sb", rowf, nc.sync)
+        rowf_sb = load_rows("rowf_sb", rowf)
         mix_sb = load_words("mix_sb", mix_words, E)
-        load_scales(mix_plane, mix_scales, nc.sync)
+        mix_plane = load_scales("mix_plane", mix_scales, E)
+
+        def deal(grouped, raw):
+            for h in range(2):
+                nc.vector.tensor_copy(
+                    out=grouped[:].rearrange("p r m j -> p m j r")[:, h * (P // 2) : (h + 1) * (P // 2), :, :],
+                    in_=raw[h][:].rearrange("p j (m r) -> p m j r", r=PACK),
+                )
+
+        def quantise(codes, plane, grouped, first, last):
+            flat = grouped[:].rearrange("p r m j -> p (r m j)")
+            nc.vector.quantize_mx(out=codes[:].bitcast(FP8X4), scales=plane[:, first:last], in_=flat[:, PACK * first : PACK * last])
+
+        def tile_codes(first, rest, r):
+            return first[:] if r == 0 else rest[:, (r - 1) * P : r * P]
 
         q_grouped = keep.tile([P, PACK, P, PACK], BF16, name="q_grouped", align_bytes=64)
-        q_first = keep.tile([P, P], U32, name="diff", align_bytes=64)
+        q_first = keep.tile([P, P], U32, name="q_first", align_bytes=64)
         q_rest = keep.tile([P, Q - P], U32, name="q_rest", align_bytes=64)
         q_plane = keep.tile([P, Q], U8, name="q_plane", align_bytes=64)
-        for h in range(2):
-            dst, src = dealt_views(q_grouped, q_raw[h], h)
-            nc.vector.tensor_copy(out=dst, in_=src)
-        q_flat = q_grouped[:].rearrange("p r m j -> p (r m j)")
-        nc.vector.quantize_mx(out=q_first[:].bitcast(FP8X4), scales=q_plane[:, :P], in_=q_flat[:, : PACK * P])
-        nc.vector.quantize_mx(out=q_rest[:].bitcast(FP8X4), scales=q_plane[:, P:], in_=q_flat[:, PACK * P :])
+        deal(q_grouped, q_raw)
+        quantise(q_first, q_plane, q_grouped, 0, P)
+        quantise(q_rest, q_plane, q_grouped, P, Q)
 
         q2_first = keep.tile([P, P], U32, name="q2_first", align_bytes=64)
         q2_rest = keep.tile([P, Q - P], U32, name="q2_rest", align_bytes=64)
         q2_plane = keep.tile([P, Q], U8, name="q2_plane", align_bytes=64)
 
-        def bank_pair(name):
-            both = psum.tile([P, 2, BANK], F32, name=name)
-            return [both[:, h, :] for h in range(2)]
-
         def single_banks(first):
             return [psum.tile([P, BANK], F32, name=f"bank{first + h}")[:] for h in range(2)]
 
+        def bank_pair(n):
+            both = psum.tile([P, 2, BANK], F32, name=f"pair{n}")
+            return [both[:, h, :] for h in range(2)]
+
         def scores(banks, r, codes, plane, moving, moving_plane):
-            rows = slice(r * P, (r + 1) * P)
             for h in range(2):
                 nc.tensor.matmul_mx(
-                    out=banks[h], lhsT=codes.bitcast(FP8X4), lhsT_scale=plane[:, rows],
+                    out=banks[h], lhsT=codes.bitcast(FP8X4), lhsT_scale=plane[:, r * P : (r + 1) * P],
                     rhs=moving(h), rhs_scale=moving_plane[:, h * BANK : (h + 1) * BANK], start=True, stop=True,
                 )
 
@@ -142,44 +142,38 @@ def tile_attend_gatedgap_threeq_mixed_kernel(
             else:
                 nc.scalar.copy(out=dst, in_=src)
 
-        def fetch(name, r, moving, moving_plane):
-            slot = (r + (name == "b")) % 2
-            codes = q_first[:] if r == 0 else q_rest[:, (r - 1) * P : r * P]
-            banks = single_banks(2 * slot) if r == 0 else bank_pair(f"pair{slot}")
-            scores(banks, r, codes, q_plane, moving, moving_plane)
-            whole = keep.tile([P, T], F32, name="first_window" if (r, name) == (0, "a") else ("b_gate0", "window")[slot])
+        def score_rows(r, side, moving, moving_plane):
+            place = (r + side) % 2
+            banks = single_banks(2 * place) if r == 0 else bank_pair(place)
+            scores(banks, r, tile_codes(q_first, q_rest, r), q_plane, moving, moving_plane)
+            whole = keep.tile([P, T], F32, name=f"window{place}")
             for h in range(2):
                 copy_out(r == 0, whole[:, h * BANK : (h + 1) * BANK], banks[h])
             return whole
 
-        def windows(r):
-            return fetch("a", r, keys_half, keys_plane), fetch("b", r, notes_half, notes_plane)
-
-        def gates(r, pair):
+        def gates(r):
+            a = score_rows(r, 0, keys_half, keys_plane)
+            b = score_rows(r, 1, notes_half, notes_plane)
             made = []
-            for name, whole, lists in (("a", pair[0], list1), ("b", pair[1], list2)):
-                s = keep.tile([P, I], F32, name=f"{name}_gate{r}")
+            for name, whole, lists in (("s1", a, list1), ("s2", b, list2)):
+                s = keep.tile([P, I], F32, name=f"{name}_{r}")
                 nc.scalar.activation(s[:], whole[:].indirect(lists[:]), ACT.Sigmoid, bias=thr_sb[:, r : r + 1], scale=slope_sb[:, r : r + 1])
                 made.append(s)
             return made
 
         def gap(r, made):
-            diff = keep.tile([P, I], F32, name=f"diff{r}")
+            diff = keep.tile([P, I], F32, name="q2_raw1" if r == 0 else f"diff{r}")
             engine = nc.vector if r == 0 else nc.gpsimd
             engine.tensor_tensor(diff[:], made[0][:], made[1][:], ALU.subtract)
             return diff
 
-        def scatter(r, diff):
-            nc.vector.tensor_copy(spread[r % 2][:].indirect(list3[:]), diff[:])
-
         def add_users(r):
-            codes = q2_first[:] if r == 0 else q2_rest[:, (r - 1) * P : r * P]
-            banks = single_banks(2 * r) if r < 2 else bank_pair(f"pair{(r + 1) % 2}")
-            scores(banks, r, codes, q2_plane, users_half, users_plane)
+            banks = single_banks(2 * r) if r < 2 else bank_pair((r + 1) % 2)
+            scores(banks, r, tile_codes(q2_first, q2_rest, r), q2_plane, users_half, users_plane)
             cc = keep.tile([P, T], F32, name=f"cc{r}")
             for h in range(2):
                 cols = slice(h * BANK, (h + 1) * BANK)
-                nc.vector.scalar_tensor_tensor(cc[:, cols], spread[r % 2][:, cols], 3.0, banks[h], ALU.mult, ALU.add)
+                nc.vector.scalar_tensor_tensor(cc[:, cols], spread[r % 2][:, cols], GAP_WEIGHT, banks[h], ALU.mult, ALU.add)
             return cc
 
         gw = keep.tile([P, I, PACK], BF16, name="gw", align_bytes=64)
@@ -192,48 +186,44 @@ def tile_attend_gatedgap_threeq_mixed_kernel(
             else:
                 nc.scalar.activation(gw[:, :, r], g, ACT.Copy, scale=factor)
 
-        made = gates(0, windows(0))
-        q2_grouped = keep.tile([P, PACK, P, PACK], BF16, name="diff", align_bytes=64)
-        for h in range(2):
-            dst, src = dealt_views(q2_grouped, q2_raw[h], h)
-            if h == 0:
-                nc.vector.tensor_copy(out=dst, in_=src)
-            else:
-                nc.gpsimd.tensor_scalar(dst, src, 1.0, 0.0, ALU.mult, ALU.add)
-        q2_flat = q2_grouped[:].rearrange("p r m j -> p (r m j)")
-        nc.vector.quantize_mx(out=q2_first[:].bitcast(FP8X4), scales=q2_plane[:, :P], in_=q2_flat[:, : PACK * P])
-        nc.vector.quantize_mx(out=q2_rest[:].bitcast(FP8X4), scales=q2_plane[:, P:], in_=q2_flat[:, PACK * P :])
-        diff = gap(0, made)
+        first_gates = gates(0)
+        q2_grouped = keep.tile([P, PACK, P, PACK], BF16, name="q_first", align_bytes=64)
+        deal(q2_grouped, q2_raw)
+        diff = gap(0, first_gates)
+        quantise(q2_first, q2_plane, q2_grouped, 0, P)
         cc_all = []
         for r in range(PACK):
-            scatter(r, diff)
+            nc.vector.tensor_copy(spread[r % 2][:].indirect(list3[:]), diff[:])
+            if r == 0:
+                quantise(q2_rest, q2_plane, q2_grouped, P, Q)
             if r + 1 < PACK:
-                diff = gap(r + 1, gates(r + 1, windows(r + 1)))
+                diff = gap(r + 1, gates(r + 1))
             cc_all.append(add_users(r))
-        g_early = keep.tile([P, PACK - 1, I], F32, name="b_gate0")
-        for r in range(PACK - 1):
-            pick(r, cc_all[r], g_early[:, r, :])
 
         last = PACK - 1
-        cc = cc_all[last]
-        g_last = keep.tile([P, I], F32, name="b_gate0")
-        nc.vector.tensor_copy(g_last[:, :HALF], cc[:].indirect(list4[:, : LIST_COLS // 2]))
-        nc.scalar.activation(g_last[:, HALF:], cc[:].indirect(list4[:, LIST_COLS // 2 :]), ACT.Copy)
-        for h in range(2):
-            slots = slice(h * HALF, (h + 1) * HALF)
-            nc.vector.tensor_scalar(gw[:, slots, last], g_last[:, slots], rowf_sb[:, last : last + 1], None, ALU.mult)
+        g_early = keep.tile([P, last, I], F32, name="window0")
+        for r in range(last):
+            pick(r, cc_all[r], g_early[:, r, :])
+
+        g_last = keep.tile([P, I], F32, name="window0")
+        nc.vector.tensor_copy(g_last[:, :HALF], cc_all[last][:].indirect(list4[:, : LIST_COLS // 2]))
+        nc.scalar.activation(g_last[:, HALF:], cc_all[last][:].indirect(list4[:, LIST_COLS // 2 :]), ACT.Copy)
+        last_factor = rowf_sb[:, last : last + 1]
+        nc.vector.tensor_scalar(gw[:, :HALF, last], g_last[:, :HALF], last_factor, None, ALU.mult)
+        nc.scalar.activation(gw[:, HALF:, last], g_last[:, HALF:], ACT.Copy, scale=last_factor)
 
         for h in range(2):
-            codes = keep.tile([P, HALF], U32, name=f"gw_codes{h}", align_bytes=64)
-            plane = keep.tile([P, HALF], U8, name=f"gw_plane{h}", align_bytes=64)
-            nc.vector.quantize_mx(out=codes[:].bitcast(FP8X4), scales=plane[:], in_=gw[:, h * HALF : (h + 1) * HALF, :].rearrange("p i r -> p (i r)"))
+            slots = slice(h * HALF, (h + 1) * HALF)
+            gw_codes = keep.tile([P, HALF], U32, name=f"gw_codes{h}", align_bytes=64)
+            gw_plane = keep.tile([P, HALF], U8, name=f"gw_plane{h}", align_bytes=64)
+            nc.vector.quantize_mx(out=gw_codes[:].bitcast(FP8X4), scales=gw_plane[:], in_=gw[:, slots, :].rearrange("p i r -> p (i r)"))
             banks = single_banks(2 * h)
             for t in range(E // P):
                 chans = slice(t * P, (t + 1) * P)
                 nc.tensor.matmul_mx(
                     out=banks[t][:, :HALF], lhsT=mix_sb[:, chans].bitcast(FP8X4), lhsT_scale=mix_plane[:, chans],
-                    rhs=codes[:].bitcast(FP8X4), rhs_scale=plane[:], start=True, stop=True,
+                    rhs=gw_codes[:].bitcast(FP8X4), rhs_scale=gw_plane[:], start=True, stop=True,
                 )
                 result = keep.tile([P, HALF], F32, name=f"result{h}{t}")
-                copy_out(h == 1 and t == 1, result[:], banks[t][:, :HALF])
-                nc.sync.dma_start(out=out[chans, h * HALF : (h + 1) * HALF], in_=result[:])
+                copy_out(h == 1 and t == E // P - 1, result[:], banks[t][:, :HALF])
+                nc.sync.dma_start(out=out[chans, slots], in_=result[:])

from contextlib import ExitStack

import concourse.mybir as mybir

D, T, I, Q, E = 512, 1024, 512, 512, 256
FLOPS = 2 * (3 * D * Q * T + Q * E * I)

F32 = mybir.dt.float32
BF16 = mybir.dt.bfloat16
I32 = mybir.dt.int32
U32 = mybir.dt.uint32
U16 = mybir.dt.uint16
U8 = mybir.dt.uint8
FP8X4 = mybir.dt.float8_e4m3fn_x4
FP4X4 = mybir.dt.float4_e2m1fn_x4
ALU = mybir.AluOpType
ACT = mybir.ActivationFunctionType

P = 128
PACK = 4
BANK = 512
HALF = I // 2
LIST_COLS = I // 16
GAP_WEIGHT = 3.0


def tile_attend_gatedgap_threeq_mixed_kernel(
    tc, query, query2, keys_words, keys_scales, notes_words, notes_scales, users_words, users_scales,
    thr, slope, rowf, mix_words, mix_scales, offs, offs2, offs3, offs4, out,
):
    nc = tc.nc
    with ExitStack() as ctx:
        keep = ctx.enter_context(tc.tile_pool(name="keep", bufs=1))
        psum = ctx.enter_context(tc.psum_pool(name="psum", bufs=1))

        def load_scales(name, scales, width):
            plane = keep.tile([P, width], U8, name=name, align_bytes=64)
            for quad in range(4):
                nc.sync.dma_start(
                    out=plane[32 * quad : 32 * quad + 4, :].bitcast(I32),
                    in_=scales[0, 4 * quad : 4 * quad + 4, :].bitcast(I32),
                )
            return plane

        def load_words(name, words, width):
            held = keep.tile([P, width], U32, name=name, align_bytes=64)
            nc.sync.dma_start(out=held[:].bitcast(I32), in_=words[0].rearrange("p n t -> p (n t)").bitcast(I32))
            return held

        def load_list(name, lists):
            held = keep.tile([P, LIST_COLS], U16, name=name)
            nc.sync.dma_start(held[:], lists)
            return held

        def load_rows(name, vec):
            held = keep.tile([P, PACK], F32, name=name)
            nc.sync.dma_start(out=held[:], in_=vec.rearrange("(p r) o -> p (r o)", r=PACK))
            return held

        def load_query_half(name, src, h):
            raw = keep.tile([P, PACK, Q // 2], F32, name=f"{name}_raw{h}")
            nc.sync.dma_start(out=raw[:], in_=src.rearrange("(p j) q -> p j q", j=PACK)[:, :, h * (Q // 2) : (h + 1) * (Q // 2)])
            return raw

        spread = []
        for n in range(2):
            zeroed = keep.tile([P, T], F32, name=f"spread{n}")
            nc.vector.memset(zeroed[:], 0.0)
            spread.append(zeroed)

        keys_plane = load_scales("keys_plane", keys_scales, T)
        q_raw = [load_query_half("q", query, h) for h in range(2)]
        slope_sb = load_rows("slope_sb", slope)
        thr_sb = load_rows("thr_sb", thr)
        list1 = load_list("list1", offs)
        keys_sb = keep.tile([P, 2 * T], U8, name="keys_sb", align_bytes=64)
        nc.sync.dma_start(out=keys_sb[:].bitcast(I32), in_=keys_words[0].bitcast(I32))
        notes_sb = load_words("notes_sb", notes_words, T)
        notes_plane = load_scales("notes_plane", notes_scales, T)
        list2 = load_list("list2", offs2)
        q2_raw = [load_query_half("q2", query2, h) for h in range(2)]
        list3 = load_list("list3", offs3)
        users_sb = load_words("users_sb", users_words, T)
        users_plane = load_scales("users_plane", users_scales, T)
        list4 = load_list("list4", offs4)
        rowf_sb = load_rows("rowf_sb", rowf)
        mix_sb = load_words("mix_sb", mix_words, E)
        mix_plane = load_scales("mix_plane", mix_scales, E)

        def deal(grouped, raw):
            for h in range(2):
                nc.vector.tensor_copy(
                    out=grouped[:].rearrange("p r m j -> p m j r")[:, h * (P // 2) : (h + 1) * (P // 2), :, :],
                    in_=raw[h][:].rearrange("p j (m r) -> p m j r", r=PACK),
                )

        def quantise(codes, plane, grouped, first, last):
            flat = grouped[:].rearrange("p r m j -> p (r m j)")
            nc.vector.quantize_mx(out=codes[:].bitcast(FP8X4), scales=plane[:, first:last], in_=flat[:, PACK * first : PACK * last])

        def tile_codes(first, rest, r):
            return first[:] if r == 0 else rest[:, (r - 1) * P : r * P]

        q_grouped = keep.tile([P, PACK, P, PACK], BF16, name="q_grouped", align_bytes=64)
        q_first = keep.tile([P, P], U32, name="q_first", align_bytes=64)
        q_rest = keep.tile([P, Q - P], U32, name="q_rest", align_bytes=64)
        q_plane = keep.tile([P, Q], U8, name="q_plane", align_bytes=64)
        deal(q_grouped, q_raw)
        quantise(q_first, q_plane, q_grouped, 0, P)
        quantise(q_rest, q_plane, q_grouped, P, Q)

        q2_first = keep.tile([P, P], U32, name="q2_first", align_bytes=64)
        q2_rest = keep.tile([P, Q - P], U32, name="q2_rest", align_bytes=64)
        q2_plane = keep.tile([P, Q], U8, name="q2_plane", align_bytes=64)

        def single_banks(first):
            return [psum.tile([P, BANK], F32, name=f"bank{first + h}")[:] for h in range(2)]

        def bank_pair(n):
            both = psum.tile([P, 2, BANK], F32, name=f"pair{n}")
            return [both[:, h, :] for h in range(2)]

        def scores(banks, r, codes, plane, moving, moving_plane):
            for h in range(2):
                nc.tensor.matmul_mx(
                    out=banks[h], lhsT=codes.bitcast(FP8X4), lhsT_scale=plane[:, r * P : (r + 1) * P],
                    rhs=moving(h), rhs_scale=moving_plane[:, h * BANK : (h + 1) * BANK], start=True, stop=True,
                )

        def keys_half(h):
            return keys_sb[:, 2 * h * BANK : 2 * (h + 1) * BANK].bitcast(FP4X4)

        def notes_half(h):
            return notes_sb[:, h * BANK : (h + 1) * BANK].bitcast(FP8X4)

        def users_half(h):
            return users_sb[:, h * BANK : (h + 1) * BANK].bitcast(FP8X4)

        def copy_out(on_vector, dst, src):
            if on_vector:
                nc.vector.tensor_copy(out=dst, in_=src)
            else:
                nc.scalar.copy(out=dst, in_=src)

        def score_rows(r, side, moving, moving_plane):
            place = (r + side) % 2
            banks = single_banks(2 * place) if r == 0 else bank_pair(place)
            scores(banks, r, tile_codes(q_first, q_rest, r), q_plane, moving, moving_plane)
            whole = keep.tile([P, T], F32, name=f"window{place}")
            for h in range(2):
                copy_out(r == 0, whole[:, h * BANK : (h + 1) * BANK], banks[h])
            return whole

        def gates(r):
            a = score_rows(r, 0, keys_half, keys_plane)
            b = score_rows(r, 1, notes_half, notes_plane)
            made = []
            for name, whole, lists in (("s1", a, list1), ("s2", b, list2)):
                s = keep.tile([P, I], F32, name=f"{name}_{r}")
                nc.scalar.activation(s[:], whole[:].indirect(lists[:]), ACT.Sigmoid, bias=thr_sb[:, r : r + 1], scale=slope_sb[:, r : r + 1])
                made.append(s)
            return made

        def gap(r, made):
            diff = keep.tile([P, I], F32, name="q2_raw1" if r == 0 else f"diff{r}")
            engine = nc.vector if r == 0 else nc.gpsimd
            engine.tensor_tensor(diff[:], made[0][:], made[1][:], ALU.subtract)
            return diff

        def add_users(r):
            banks = single_banks(2 * r) if r < 2 else bank_pair((r + 1) % 2)
            scores(banks, r, tile_codes(q2_first, q2_rest, r), q2_plane, users_half, users_plane)
            cc = keep.tile([P, T], F32, name=f"cc{r}")
            for h in range(2):
                cols = slice(h * BANK, (h + 1) * BANK)
                nc.vector.scalar_tensor_tensor(cc[:, cols], spread[r % 2][:, cols], GAP_WEIGHT, banks[h], ALU.mult, ALU.add)
            return cc

        gw = keep.tile([P, I, PACK], BF16, name="gw", align_bytes=64)

        def pick(r, cc, g):
            factor = rowf_sb[:, r : r + 1]
            nc.scalar.activation(g, cc[:].indirect(list4[:]), ACT.Copy)
            if r < 2:
                nc.gpsimd.tensor_scalar(gw[:, :, r], g, factor, 0.0, ALU.mult, ALU.add)
            else:
                nc.scalar.activation(gw[:, :, r], g, ACT.Copy, scale=factor)

        first_gates = gates(0)
        q2_grouped = keep.tile([P, PACK, P, PACK], BF16, name="q_first", align_bytes=64)
        deal(q2_grouped, q2_raw)
        diff = gap(0, first_gates)
        quantise(q2_first, q2_plane, q2_grouped, 0, P)
        cc_all = []
        for r in range(PACK):
            nc.vector.tensor_copy(spread[r % 2][:].indirect(list3[:]), diff[:])
            if r == 0:
                quantise(q2_rest, q2_plane, q2_grouped, P, Q)
            if r + 1 < PACK:
                diff = gap(r + 1, gates(r + 1))
            cc_all.append(add_users(r))

        last = PACK - 1
        g_early = keep.tile([P, last, I], F32, name="window0")
        for r in range(last):
            pick(r, cc_all[r], g_early[:, r, :])

        g_last = keep.tile([P, I], F32, name="window0")
        nc.vector.tensor_copy(g_last[:, :HALF], cc_all[last][:].indirect(list4[:, : LIST_COLS // 2]))
        nc.scalar.activation(g_last[:, HALF:], cc_all[last][:].indirect(list4[:, LIST_COLS // 2 :]), ACT.Copy)
        last_factor = rowf_sb[:, last : last + 1]
        nc.vector.tensor_scalar(gw[:, :HALF, last], g_last[:, :HALF], last_factor, None, ALU.mult)
        nc.scalar.activation(gw[:, HALF:, last], g_last[:, HALF:], ACT.Copy, scale=last_factor)

        for h in range(2):
            slots = slice(h * HALF, (h + 1) * HALF)
            gw_codes = keep.tile([P, HALF], U32, name=f"gw_codes{h}", align_bytes=64)
            gw_plane = keep.tile([P, HALF], U8, name=f"gw_plane{h}", align_bytes=64)
            nc.vector.quantize_mx(out=gw_codes[:].bitcast(FP8X4), scales=gw_plane[:], in_=gw[:, slots, :].rearrange("p i r -> p (i r)"))
            banks = single_banks(2 * h)
            for t in range(E // P):
                chans = slice(t * P, (t + 1) * P)
                nc.tensor.matmul_mx(
                    out=banks[t][:, :HALF], lhsT=mix_sb[:, chans].bitcast(FP8X4), lhsT_scale=mix_plane[:, chans],
                    rhs=gw_codes[:].bitcast(FP8X4), rhs_scale=gw_plane[:], start=True, stop=True,
                )
                result = keep.tile([P, HALF], F32, name=f"result{h}{t}")
                copy_out(h == 1 and t == E // P - 1, result[:], banks[t][:, :HALF])
                nc.sync.dma_start(out=out[chans, slots], in_=result[:])
